import numpy as np
import ml_dtypes


def mxq(x, axis, fmt="e4m3"):
    dtype, down = {"e4m3": (ml_dtypes.float8_e4m3fn, 7), "e5m2": (ml_dtypes.float8_e5m2, 14)}[fmt]
    v = np.moveaxis(np.asarray(x, np.float32).astype(ml_dtypes.bfloat16).astype(np.float64), axis, -1)
    blocks = v.reshape(v.shape[:-1] + (-1, 32))
    amax = np.abs(blocks).max(-1, keepdims=True)
    byte = np.maximum(np.where(amax > 0, np.frexp(amax)[1] - 1 + 127, 0) - down, 1)
    scale = np.exp2(byte - 127.0)
    codes = (blocks / scale).astype(np.float32).astype(dtype).astype(np.float64)
    return np.moveaxis((codes * scale).reshape(v.shape), -1, axis)


WIDE = False


def mx_kscale(k):
    if not WIDE:
        return np.ones(k)
    levels = np.array([24, -24, 12, -12, 0])
    if k % 512:
        return np.exp2(np.random.permutation(np.resize(levels, k // 32))).repeat(32)
    a = np.empty((k // 512, 16))
    for p in range(k // 512):
        a[p, :8] = np.random.permutation(np.resize(levels, 8))
        for g in range(8):
            far = levels[np.abs(levels - a[p, g]) >= 10]
            a[p, g + 8] = far[np.random.randint(len(far))]
    return np.exp2(a.ravel()).repeat(32)


def f64(x):
    return np.asarray(x).astype(np.float64)


def striped(idx):
    return np.tile(idx.reshape(-1, 16).T, (8, 1)).astype(np.uint16)


def unstriped(offs):
    return offs[:16].T.reshape(-1).astype(np.int64)


E2M1 = np.array([0.0, 0.5, 1.0, 1.5, 2.0, 3.0, 4.0, 6.0, -0.0, -0.5, -1.0, -1.5, -2.0, -3.0, -4.0, -6.0])


def pack_weight(w, fmt):
    k, n = w.shape
    w = f64(np.asarray(w, np.float32).astype(ml_dtypes.bfloat16)).reshape(k // 32, 32, n)
    amax = np.abs(w).max(1)
    if fmt == "e4m3":
        byte = np.frexp(amax)[1] - 1 + 127 - 7
    else:
        mant, ex = np.frexp(amax / 6.0)
        byte = np.where(mant > 0.5, ex, ex - 1) + 127
    byte = np.clip(np.where(amax > 0, byte, 1), 1, 254)
    scaled = (w * np.exp2(127.0 - byte)[:, None, :]).reshape(k, n).astype(np.float32)
    by_word = np.ascontiguousarray(scaled.reshape(k // 512, 128, 4, n).transpose(0, 1, 3, 2))
    if fmt == "e4m3":
        words = by_word.astype(ml_dtypes.float8_e4m3fn).view(np.uint8)
    else:
        c = by_word.astype(ml_dtypes.float4_e2m1fn).view(np.uint8) & 0xF
        words = (c[..., 0::2] | (c[..., 1::2] << 4)).reshape(k // 512, 128, 2 * n)
    return np.ascontiguousarray(words), np.ascontiguousarray(byte.astype(np.uint8).reshape(k // 512, 16, n))


def unpack_weight(words, scales, fmt):
    g, _, n = scales.shape
    words = np.ascontiguousarray(words).reshape(g, 128, n, -1)
    if fmt == "e4m3":
        vals = words.view(ml_dtypes.float8_e4m3fn).astype(np.float64)
    else:
        nib = np.empty((g, 128, n, 4), np.uint8)
        nib[..., 0::2] = words & 0xF
        nib[..., 1::2] = words >> 4
        vals = E2M1[nib]
    vals = vals * np.repeat(np.exp2(scales.astype(np.float64) - 127.0), 8, axis=1)[..., None]
    return vals.transpose(0, 1, 3, 2).reshape(g * 512, n)


def planes(y):
    n, m = y.shape
    v = y.astype(np.float32).astype(ml_dtypes.bfloat16).astype(np.float64).reshape(n // 32, 32, m)
    top = np.abs(v).max(1)
    byte = np.clip(np.where(top > 0, np.frexp(top)[1] - 1 + 127 - 7, 1), 1, 254)
    codes = (v * np.exp2(127.0 - byte)[:, None, :]).reshape(n, m).astype(np.float32).astype(ml_dtypes.float8_e4m3fn).view(np.uint8)
    words = codes.reshape(n // 512, 128, 4, m).transpose(0, 1, 3, 2)
    return np.ascontiguousarray(words), np.ascontiguousarray(byte.astype(np.uint8).reshape(n // 512, 16, m))


K, R, N, T, J = 1024, 512, 512, 2048, 1024


def setup_inputs():
    n = np.random.standard_normal
    s = mx_kscale(K)[:, None]
    u = mx_kscale(R)[:, None]
    p_tab = pack_weight(n((K, T)) * s, "e4m3")
    p_ws = pack_weight(n((K, R)) / np.sqrt(2 * K) / s * u.T, "e4m3")
    p_wt = pack_weight(n((K, R)) / np.sqrt(2 * K) / s * u.T, "e2m1")
    return {
        "tab_words": p_tab[0],
        "tab_scales": p_tab[1],
        "ws_words": p_ws[0],
        "ws_scales": p_ws[1],
        "wt_words": p_wt[0],
        "wt_scales": p_wt[1],
        "wd": (n((R, N)) / np.sqrt(R) / u).astype(np.float32),
        "rT": (n((N, T))).astype(np.float32),
        "wgo": np.tile(np.random.uniform(0.5, 2.0, J), (128, 1)).astype(np.float32),
        "offs": striped(np.random.permutation(T)[:J]),
        "offs2": striped(np.random.permutation(T)[:J]),
    }


def reference(tab_words, tab_scales, ws_words, ws_scales, wt_words, wt_scales, wd, rT, wgo, offs, offs2):
    idx = unstriped(offs)
    idx2 = unstriped(offs2)
    tab_ = unpack_weight(tab_words, tab_scales, "e4m3")[:, idx]
    tabb_ = unpack_weight(tab_words, tab_scales, "e4m3")[:, idx2]
    ws_ = unpack_weight(ws_words, ws_scales, "e4m3")
    wt_ = unpack_weight(wt_words, wt_scales, "e2m1")
    a = ws_.T @ tab_ + wt_.T @ tabb_
    h = a
    h_ = mxq(h, 0, "e4m3")
    wd_ = mxq(f64(wd), 0, "e4m3")
    y = wd_.T @ h_
    out = np.zeros((N, T))
    out[:, idx2] = f64(wgo)[0] * (y + f64(rT)[:, idx2])
    return (out,) + planes(out)

@@ -1,0 +1,245 @@
+from contextlib import ExitStack
+
+import concourse.mybir as mybir
+
+K, R, N, T, J = 1024, 512, 512, 2048, 1024
+FLOPS = 2 * (2 * K * R * J + R * N * J)
+
+F32 = mybir.dt.float32
+BF16 = mybir.dt.bfloat16
+I32 = mybir.dt.int32
+U32 = mybir.dt.uint32
+U16 = mybir.dt.uint16
+U8 = mybir.dt.uint8
+FP8X4 = mybir.dt.float8_e4m3fn_x4
+FP4X4 = mybir.dt.float4_e2m1fn_x4
+ADD = mybir.AluOpType.add
+MULT = mybir.AluOpType.mult
+
+P = 128
+PASSES = K // 512
+CHUNK = 256
+CHUNKS = J // CHUNK
+SUB = 128
+OUT_CHUNK = 512
+OUT_CHUNKS = T // OUT_CHUNK
+VECTOR_ROUNDS = 2
+PAGE_ORDER = (2, 0, 1, 3)
+
+
+def tile_list_msg_none_resLP_kernel(
+    tc, tab_words, tab_scales, ws_words, ws_scales, wt_words, wt_scales, wd, rT, wgo, offs, offs2,
+    out_0, out_1, out_2,
+):
+    nc = tc.nc
+    with ExitStack() as ctx:
+        keep = ctx.enter_context(tc.tile_pool(name="keep", bufs=1))
+        ring = ctx.enter_context(tc.tile_pool(name="ring", bufs=2))
+        psum_a = ctx.enter_context(tc.psum_pool(name="psum_a", bufs=4))
+        psum_y = ctx.enter_context(tc.psum_pool(name="psum_y", bufs=4))
+
+        tab_plane = keep.tile([P, T], U8, name="tab_plane", align_bytes=64)
+        w_plane_raw = keep.tile([P, 2 * PASSES * R], U8, name="w_plane_raw", align_bytes=64)
+        dst_plane_1 = keep.tile([P, J], U8, name="dst_plane_1", align_bytes=64)
+        for plane in (tab_plane, w_plane_raw, dst_plane_1):
+            nc.vector.memset(plane[:].bitcast(I32), 0)
+        page_pool = ctx.enter_context(tc.tile_pool(name="pages", bufs=3))
+        pages = {}
+        for i in PAGE_ORDER[:3]:
+            pages[i] = page_pool.tile([P, T], F32, name="page")
+            nc.vector.memset(pages[i][:].bitcast(I32), 0)
+
+        dst_list = keep.tile([P, J // 16], U16, name="dst_list")
+        src_list = keep.tile([P, J // 16], U16, name="src_list")
+        nc.sync.dma_start(dst_list[:], offs2)
+        nc.sync.dma_start(src_list[:], offs)
+
+        tab = [keep.tile([P, T], U32, name=f"tab{a}", align_bytes=64) for a in range(PASSES)]
+
+        def load_tab(a):
+            nc.sync.dma_start(tab[a][:].bitcast(I32), tab_words[a].rearrange("p t i -> p (t i)").bitcast(I32))
+
+        load_tab(0)
+        for q in range(4):
+            nc.sync.dma_start(
+                tab_plane[32 * q : 32 * q + 4 * PASSES, :].bitcast(I32),
+                tab_scales[:, 4 * q : 4 * q + 4, :].bitcast(I32),
+            )
+        load_tab(1)
+
+        ws_raw = keep.tile([P, PASSES, R], U32, name="ws_raw")
+        wt_raw = keep.tile([P, PASSES, R // 2], U32, name="wt_raw")
+        nc.sync.dma_start(ws_raw[:].bitcast(I32), ws_words.rearrange("a p r i -> p a (r i)").bitcast(I32))
+        nc.sync.dma_start(wt_raw[:].bitcast(I32), wt_words.rearrange("a p b -> p a b").bitcast(I32))
+        for w, scales in enumerate((ws_scales, wt_scales)):
+            for q in range(4):
+                nc.sync.dma_start(
+                    w_plane_raw[32 * q : 32 * q + 4, w * PASSES * R : (w + 1) * PASSES * R]
+                    .bitcast(I32)
+                    .rearrange("p (a r) -> p a r", a=PASSES),
+                    scales[:, 4 * q : 4 * q + 4, :].bitcast(I32).rearrange("a q r -> q a r"),
+                )
+
+        dst_plane = keep.tile([P, J], U8, name="dst_plane", align_bytes=64)
+        src_plane = keep.tile([P, J], U8, name="src_plane", align_bytes=64)
+        nc.vector.tensor_copy(dst_plane[:], tab_plane[:].indirect(dst_list[:]))
+        nc.vector.tensor_copy(src_plane[:], tab_plane[:].indirect(src_list[:]))
+        for q in range(4):
+            nc.sync.dma_start(
+                dst_plane_1[32 * q : 32 * q + 4, :].bitcast(I32),
+                dst_plane[32 * q + 4 : 32 * q + 8, :].bitcast(I32),
+            )
+
+        wd_raw = keep.tile([P, 4, N], F32, name="wd_raw")
+        wd_rows = wd.rearrange("(q i u) n -> i q u n", i=4, u=8)
+        for i in range(4):
+            nc.sync.dma_start(wd_raw[:, i, :], wd_rows[i])
+        wgo_sb = keep.tile([P, J], F32, name="wgo_sb")
+        res = [keep.tile([P, T], F32, name=f"res{i}") for i in range(4)]
+        res_rows = rT.rearrange("(p i) t -> i p t", i=4)
+        nc.sync.dma_start(res[PAGE_ORDER[0]][:], res_rows[PAGE_ORDER[0]])
+        nc.sync.dma_start(wgo_sb[:], wgo)
+        for i in PAGE_ORDER[1:]:
+            nc.sync.dma_start(res[i][:], res_rows[i])
+
+        ws_codes = keep.tile([P, PASSES, R], U32, name="ws_codes", align_bytes=64)
+        wt_codes = keep.tile([P, PASSES, R // 2], U32, name="wt_codes", align_bytes=64)
+        w_plane = keep.tile([P, 2 * PASSES * R], U8, name="w_plane", align_bytes=64)
+        for a in range(PASSES):
+            nc.scalar.copy(
+                ws_codes[:, a, :].rearrange("p (i q u) -> p i q u", i=4, u=8),
+                ws_raw[:, a, :].rearrange("p (q i u) -> p i q u", i=4, u=8),
+            )
+            nc.scalar.copy(
+                wt_codes[:, a, :].rearrange("p (i q u) -> p i q u", i=4, u=4),
+                wt_raw[:, a, :].rearrange("p (q i u) -> p i q u", i=4, u=4),
+            )
+        nc.scalar.copy(
+            w_plane[:].bitcast(U32).rearrange("p (s i q u) -> p s i q u", i=4, q=16, u=2),
+            w_plane_raw[:].bitcast(U32).rearrange("p (s q i u) -> p s i q u", i=4, q=16, u=2),
+        )
+
+        wd_bf = keep.tile([P, 4 * N], BF16, name="wd_bf", align_bytes=64)
+        wd_codes = keep.tile([P, N], U32, name="wd_codes", align_bytes=64)
+        wd_plane = keep.tile([P, N], U8, name="wd_plane", align_bytes=64)
+        nc.scalar.copy(
+            wd_bf[:].rearrange("p (s m i) -> p m s i", s=4, i=4),
+            wd_raw[:].rearrange("p i (m s) -> p m s i", s=4),
+        )
+        nc.vector.quantize_mx(out=wd_codes[:].bitcast(FP8X4), scales=wd_plane[:], in_=wd_bf[:])
+
+        y = keep.tile([P, 4, J], F32, name="y")
+        total = [keep.tile([P, J], F32, name=f"total{i}") for i in range(4)]
+
+        def first_stage(c):
+            offsets = slice(c * CHUNK // 16, (c + 1) * CHUNK // 16)
+            picked = {}
+            for a in range(PASSES):
+                for side, lst in (("src", src_list), ("dst", dst_list)):
+                    g = ring.tile([P, CHUNK], U32, name=f"{side}{a}", align_bytes=64)
+                    nc.vector.tensor_copy(g[:], tab[a][:].indirect(lst[:, offsets]))
+                    picked[side, a] = g
+            h_bf = ring.tile([P, 4 * CHUNK], BF16, name="h_bf", align_bytes=64)
+            banks = [psum_a.tile([P, 4, SUB], F32, name="acc") for b in range(CHUNK // SUB)]
+            steps = [(a, side) for a in range(PASSES) for side in ("src", "dst")]
+            for n, (a, side) in enumerate(steps):
+                for b, acc in enumerate(banks):
+                    cols = slice(b * SUB, (b + 1) * SUB)
+                    edges = slice(c * CHUNK + b * SUB, c * CHUNK + (b + 1) * SUB)
+                    for i in range(4):
+                        if side == "src":
+                            lhsT = ws_codes[:, a, i * P : (i + 1) * P].bitcast(FP8X4)
+                            first = a * R + i * P
+                            rhs_scale = src_plane[4 * a : P, edges]
+                        else:
+                            lhsT = wt_codes[:, a, i * P // 2 : (i + 1) * P // 2].bitcast(U8).bitcast(FP4X4)
+                            first = (PASSES + a) * R + i * P
+                            rhs_scale = (dst_plane, dst_plane_1)[a][:, edges]
+                        nc.tensor.matmul_mx(
+                            out=acc[:, i, :],
+                            lhsT=lhsT,
+                            lhsT_scale=w_plane[:, first : first + P],
+                            rhs=picked[side, a][:, cols].bitcast(FP8X4),
+                            rhs_scale=rhs_scale,
+                            start=(n == 0 and i == 0),
+                            stop=(n == len(steps) - 1 and i == 3),
+                        )
+            for b, acc in enumerate(banks):
+                nc.scalar.copy(
+                    h_bf[:, 4 * b * SUB : 4 * (b + 1) * SUB].rearrange("p (j i) -> p j i", i=4),
+                    acc[:].rearrange("p i j -> p j i"),
+                )
+            return h_bf
+
+        def second_stage(c, h_bf):
+            h_codes = ring.tile([P, CHUNK], U32, name="h_codes", align_bytes=64)
+            h_plane = ring.tile([P, CHUNK], U8, name="h_plane", align_bytes=64)
+            nc.vector.quantize_mx(out=h_codes[:].bitcast(FP8X4), scales=h_plane[:], in_=h_bf[:])
+            edges = slice(c * CHUNK, (c + 1) * CHUNK)
+            for pair in range(2):
+                acc = psum_y.tile([P, 2, CHUNK], F32, name="acc_y")
+                for s in range(2):
+                    i = 2 * pair + s
+                    nc.tensor.matmul_mx(
+                        out=acc[:, s, :],
+                        lhsT=wd_codes[:, i * P : (i + 1) * P].bitcast(FP8X4),
+                        lhsT_scale=wd_plane[:, i * P : (i + 1) * P],
+                        rhs=h_codes[:].bitcast(FP8X4),
+                        rhs_scale=h_plane[:],
+                        start=True,
+                        stop=True,
+                    )
+                nc.scalar.copy(y[:, 2 * pair : 2 * pair + 2, edges], acc[:])
+
+        pending = None
+        for c in range(CHUNKS):
+            h_bf = first_stage(c)
+            if pending is not None:
+                second_stage(*pending)
+            pending = (c, h_bf)
+        second_stage(*pending)
+
+        def add_state(i):
+            for c in range(CHUNKS):
+                edges = slice(c * CHUNK, (c + 1) * CHUNK)
+                offsets = slice(c * CHUNK // 16, (c + 1) * CHUNK // 16)
+                nc.vector.tensor_tensor(total[i][:, edges], res[i][:].indirect(dst_list[:, offsets]), y[:, i, edges], ADD)
+
+        rounded = [keep.tile([P, OUT_CHUNK, 4], BF16, name=f"rounded{c}", align_bytes=64) for c in range(OUT_CHUNKS)]
+        out_rows = out_0.rearrange("(p i) t -> i p t", i=4)
+
+        def place(i):
+            if i not in pages:
+                pages[i] = page_pool.tile([P, T], F32, name="page")
+                nc.gpsimd.memset(pages[i][:], 0.0)
+            nc.vector.tensor_tensor(pages[i][:].indirect(dst_list[:]), total[i][:], wgo_sb[:], MULT)
+            nc.sync.dma_start(out_rows[i], pages[i][:])
+            for c in range(OUT_CHUNKS):
+                src = pages[i][:, c * OUT_CHUNK : (c + 1) * OUT_CHUNK]
+                if i == 3 and c < VECTOR_ROUNDS:
+                    nc.vector.tensor_copy(rounded[c][:, :, i], src)
+                else:
+                    nc.scalar.copy(rounded[c][:, :, i], src)
+
+        add_state(PAGE_ORDER[0])
+        for n, i in enumerate(PAGE_ORDER):
+            if n + 1 < 4:
+                add_state(PAGE_ORDER[n + 1])
+            place(i)
+
+        out_plane = keep.tile([P, T], U8, name="out_plane", align_bytes=64)
+        out_words = out_1[0].rearrange("p t i -> p (t i)").bitcast(I32)
+        for c in range(OUT_CHUNKS):
+            cols = slice(c * OUT_CHUNK, (c + 1) * OUT_CHUNK)
+            out_codes = keep.tile([P, OUT_CHUNK], U32, name=f"out_codes{c}", align_bytes=64)
+            nc.vector.quantize_mx(
+                out=out_codes[:].bitcast(FP8X4),
+                scales=out_plane[:, cols],
+                in_=rounded[c][:].rearrange("p t i -> p (t i)"),
+            )
+            nc.sync.dma_start(out_words[:, cols], out_codes[:].bitcast(I32))
+        for q in range(4):
+            nc.scalar.dma_start(
+                out_2[0, 4 * q : 4 * q + 4, :].bitcast(I32),
+                out_plane[32 * q : 32 * q + 4, :].bitcast(I32),
+            )

@@ -38,15 +38,14 @@ def tile_list_msg_none_resLP_kernel(
         psum_a = ctx.enter_context(tc.psum_pool(name="psum_a", bufs=4))
         psum_y = ctx.enter_context(tc.psum_pool(name="psum_y", bufs=4))
 
-        tab_plane = keep.tile([P, T], U8, name="tab_plane", align_bytes=64)
-        w_plane_raw = keep.tile([P, 2 * PASSES * R], U8, name="w_plane_raw", align_bytes=64)
+        tab_plane = keep.tile([P, T], U8, name="tab_plane", tag="tab_plane", align_bytes=64)
+        w_plane_raw = [keep.tile([P, PASSES * R], U8, name=f"w_plane_raw{w}", align_bytes=64) for w in range(2)]
         dst_plane_1 = keep.tile([P, J], U8, name="dst_plane_1", align_bytes=64)
-        for plane in (tab_plane, w_plane_raw, dst_plane_1):
+        for plane in (tab_plane, *w_plane_raw, dst_plane_1):
             nc.vector.memset(plane[:].bitcast(I32), 0)
-        page_pool = ctx.enter_context(tc.tile_pool(name="pages", bufs=3))
         pages = {}
-        for i in PAGE_ORDER[:3]:
-            pages[i] = page_pool.tile([P, T], F32, name="page")
+        for n, i in enumerate(PAGE_ORDER[:2]):
+            pages[i] = keep.tile([P, T], F32, name=f"page{i}", tag=f"page_slot{n}")
             nc.vector.memset(pages[i][:].bitcast(I32), 0)
 
         dst_list = keep.tile([P, J // 16], U16, name="dst_list")
@@ -65,7 +64,6 @@ def tile_list_msg_none_resLP_kernel(
                 tab_plane[32 * q : 32 * q + 4 * PASSES, :].bitcast(I32),
                 tab_scales[:, 4 * q : 4 * q + 4, :].bitcast(I32),
             )
-        load_tab(1)
 
         ws_raw = keep.tile([P, PASSES, R], U32, name="ws_raw")
         wt_raw = keep.tile([P, PASSES, R // 2], U32, name="wt_raw")
@@ -73,15 +71,32 @@ def tile_list_msg_none_resLP_kernel(
         nc.sync.dma_start(wt_raw[:].bitcast(I32), wt_words.rearrange("a p b -> p a b").bitcast(I32))
         for w, scales in enumerate((ws_scales, wt_scales)):
             for q in range(4):
+                if (w, q) == (1, 2):
+                    load_tab(1)
                 nc.sync.dma_start(
-                    w_plane_raw[32 * q : 32 * q + 4, w * PASSES * R : (w + 1) * PASSES * R]
-                    .bitcast(I32)
-                    .rearrange("p (a r) -> p a r", a=PASSES),
+                    w_plane_raw[w][32 * q : 32 * q + 4, :].bitcast(I32).rearrange("p (a r) -> p a r", a=PASSES),
                     scales[:, 4 * q : 4 * q + 4, :].bitcast(I32).rearrange("a q r -> q a r"),
                 )
 
         dst_plane = keep.tile([P, J], U8, name="dst_plane", align_bytes=64)
         src_plane = keep.tile([P, J], U8, name="src_plane", align_bytes=64)
+        picked = {}
+
+        def pick(c, a):
+            offsets = slice(c * CHUNK // 16, (c + 1) * CHUNK // 16)
+            width = 2 * PASSES * CHUNK
+            if a == 0 and c == 1:
+                middle = keep.tile([P, 2 * width], U32, name="picked_middle", tag="tab_plane", align_bytes=64)
+                picked[1], picked[2] = middle[:, :width], middle[:, width:]
+            elif a == 0 and c != 2:
+                tag = "h_bf0" if c == CHUNKS - 1 else "picked_first"
+                picked[c] = keep.tile([P, width], U32, name=f"picked{c}", tag=tag, align_bytes=64)
+            for n, (side, lst) in enumerate((("src", src_list), ("dst", dst_list))):
+                g = picked[c][:, (2 * a + n) * CHUNK : (2 * a + n + 1) * CHUNK]
+                nc.vector.tensor_copy(g, tab[a][:].indirect(lst[:, offsets]))
+                picked[side, a, c] = g
+
+        pick(0, 0)
         nc.vector.tensor_copy(dst_plane[:], tab_plane[:].indirect(dst_list[:]))
         nc.vector.tensor_copy(src_plane[:], tab_plane[:].indirect(src_list[:]))
         for q in range(4):
@@ -95,51 +110,45 @@ def tile_list_msg_none_resLP_kernel(
         for i in range(4):
             nc.sync.dma_start(wd_raw[:, i, :], wd_rows[i])
         wgo_sb = keep.tile([P, J], F32, name="wgo_sb")
-        res = [keep.tile([P, T], F32, name=f"res{i}") for i in range(4)]
+        res = [keep.tile([P, T], F32, name=f"res{i}", tag=f"res_slot{i}") for i in range(4)]
         res_rows = rT.rearrange("(p i) t -> i p t", i=4)
-        nc.sync.dma_start(res[PAGE_ORDER[0]][:], res_rows[PAGE_ORDER[0]])
-        nc.sync.dma_start(wgo_sb[:], wgo)
-        for i in PAGE_ORDER[1:]:
+        for i in PAGE_ORDER[:3]:
             nc.sync.dma_start(res[i][:], res_rows[i])
+        nc.sync.dma_start(wgo_sb[:], wgo)
+        nc.sync.dma_start(res[PAGE_ORDER[3]][:], res_rows[PAGE_ORDER[3]])
 
         ws_codes = keep.tile([P, PASSES, R], U32, name="ws_codes", align_bytes=64)
         wt_codes = keep.tile([P, PASSES, R // 2], U32, name="wt_codes", align_bytes=64)
-        w_plane = keep.tile([P, 2 * PASSES * R], U8, name="w_plane", align_bytes=64)
-        for a in range(PASSES):
+        w_plane = [keep.tile([P, PASSES * R], U8, name=f"w_plane{w}", align_bytes=64) for w in range(2)]
+        for w, (codes, raw) in enumerate(((ws_codes, ws_raw), (wt_codes, wt_raw))):
             nc.scalar.copy(
-                ws_codes[:, a, :].rearrange("p (i q u) -> p i q u", i=4, u=8),
-                ws_raw[:, a, :].rearrange("p (q i u) -> p i q u", i=4, u=8),
+                codes[:].rearrange("p a (i q u) -> p a i q u", i=4, q=16),
+                raw[:].rearrange("p a (q i u) -> p a i q u", i=4, q=16),
             )
             nc.scalar.copy(
-                wt_codes[:, a, :].rearrange("p (i q u) -> p i q u", i=4, u=4),
-                wt_raw[:, a, :].rearrange("p (q i u) -> p i q u", i=4, u=4),
+                w_plane[w][:].bitcast(U32).rearrange("p (a i q u) -> p a i q u", a=PASSES, i=4, q=16),
+                w_plane_raw[w][:].bitcast(U32).rearrange("p (a q i u) -> p a i q u", a=PASSES, i=4, q=16),
             )
-        nc.scalar.copy(
-            w_plane[:].bitcast(U32).rearrange("p (s i q u) -> p s i q u", i=4, q=16, u=2),
-            w_plane_raw[:].bitcast(U32).rearrange("p (s q i u) -> p s i q u", i=4, q=16, u=2),
-        )
 
         wd_bf = keep.tile([P, 4 * N], BF16, name="wd_bf", align_bytes=64)
         wd_codes = keep.tile([P, N], U32, name="wd_codes", align_bytes=64)
         wd_plane = keep.tile([P, N], U8, name="wd_plane", align_bytes=64)
-        nc.scalar.copy(
-            wd_bf[:].rearrange("p (s m i) -> p m s i", s=4, i=4),
-            wd_raw[:].rearrange("p i (m s) -> p m s i", s=4),
-        )
+        for half in range(2):
+            ms = slice(half * P // 2, (half + 1) * P // 2)
+            nc.scalar.copy(
+                wd_bf[:].rearrange("p (s m i) -> p m s i", s=4, i=4)[:, ms],
+                wd_raw[:].rearrange("p i (m s) -> p m s i", s=4)[:, ms],
+            )
         nc.vector.quantize_mx(out=wd_codes[:].bitcast(FP8X4), scales=wd_plane[:], in_=wd_bf[:])
 
         y = keep.tile([P, 4, J], F32, name="y")
-        total = [keep.tile([P, J], F32, name=f"total{i}") for i in range(4)]
+        total = {i: keep.tile([P, J], F32, name=f"total{i}", tag=f"total_slot{n}") for n, i in enumerate(PAGE_ORDER[:3])}
 
         def first_stage(c):
-            offsets = slice(c * CHUNK // 16, (c + 1) * CHUNK // 16)
-            picked = {}
             for a in range(PASSES):
-                for side, lst in (("src", src_list), ("dst", dst_list)):
-                    g = ring.tile([P, CHUNK], U32, name=f"{side}{a}", align_bytes=64)
-                    nc.vector.tensor_copy(g[:], tab[a][:].indirect(lst[:, offsets]))
-                    picked[side, a] = g
-            h_bf = ring.tile([P, 4 * CHUNK], BF16, name="h_bf", align_bytes=64)
+                if ("src", a, c) not in picked:
+                    pick(c, a)
+            h_bf = keep.tile([P, 4 * CHUNK], BF16, name=f"h_bf{c}", tag=f"h_bf{c}", align_bytes=64)
             banks = [psum_a.tile([P, 4, SUB], F32, name="acc") for b in range(CHUNK // SUB)]
             steps = [(a, side) for a in range(PASSES) for side in ("src", "dst")]
             for n, (a, side) in enumerate(steps):
@@ -149,17 +158,17 @@ def tile_list_msg_none_resLP_kernel(
                     for i in range(4):
                         if side == "src":
                             lhsT = ws_codes[:, a, i * P : (i + 1) * P].bitcast(FP8X4)
-                            first = a * R + i * P
+                            lhsT_plane = w_plane[0]
                             rhs_scale = src_plane[4 * a : P, edges]
                         else:
                             lhsT = wt_codes[:, a, i * P // 2 : (i + 1) * P // 2].bitcast(U8).bitcast(FP4X4)
-                            first = (PASSES + a) * R + i * P
+                            lhsT_plane = w_plane[1]
                             rhs_scale = (dst_plane, dst_plane_1)[a][:, edges]
                         nc.tensor.matmul_mx(
                             out=acc[:, i, :],
                             lhsT=lhsT,
-                            lhsT_scale=w_plane[:, first : first + P],
-                            rhs=picked[side, a][:, cols].bitcast(FP8X4),
+                            lhsT_scale=lhsT_plane[:, a * R + i * P : a * R + (i + 1) * P],
+                            rhs=picked[side, a, c][:, cols].bitcast(FP8X4),
                             rhs_scale=rhs_scale,
                             start=(n == 0 and i == 0),
                             stop=(n == len(steps) - 1 and i == 3),
@@ -179,7 +188,7 @@ def tile_list_msg_none_resLP_kernel(
             for pair in range(2):
                 acc = psum_y.tile([P, 2, CHUNK], F32, name="acc_y")
                 for s in range(2):
-                    i = 2 * pair + s
+                    i = PAGE_ORDER[2 * pair + s]
                     nc.tensor.matmul_mx(
                         out=acc[:, s, :],
                         lhsT=wd_codes[:, i * P : (i + 1) * P].bitcast(FP8X4),
@@ -199,33 +208,41 @@ def tile_list_msg_none_resLP_kernel(
             pending = (c, h_bf)
         second_stage(*pending)
 
-        def add_state(i):
-            for c in range(CHUNKS):
-                edges = slice(c * CHUNK, (c + 1) * CHUNK)
-                offsets = slice(c * CHUNK // 16, (c + 1) * CHUNK // 16)
-                nc.vector.tensor_tensor(total[i][:, edges], res[i][:].indirect(dst_list[:, offsets]), y[:, i, edges], ADD)
+        def add_state(i, first, count):
+            edges = slice(first, first + count)
+            offsets = slice(first // 16, (first + count) // 16)
+            nc.vector.tensor_tensor(total[i][:, edges], res[i][:].indirect(dst_list[:, offsets]), y[:, PAGE_ORDER.index(i), edges], ADD)
 
-        rounded = [keep.tile([P, OUT_CHUNK, 4], BF16, name=f"rounded{c}", align_bytes=64) for c in range(OUT_CHUNKS)]
+        rounded = keep.tile([P, T, 4], BF16, name="rounded", align_bytes=64)
         out_rows = out_0.rearrange("(p i) t -> i p t", i=4)
 
         def place(i):
             if i not in pages:
-                pages[i] = page_pool.tile([P, T], F32, name="page")
+                slot = "page_slot0" if i == PAGE_ORDER[3] else f"res_slot{PAGE_ORDER[0]}"
+                pages[i] = keep.tile([P, T], F32, name=f"page{i}", tag=slot)
                 nc.gpsimd.memset(pages[i][:], 0.0)
             nc.vector.tensor_tensor(pages[i][:].indirect(dst_list[:]), total[i][:], wgo_sb[:], MULT)
             nc.sync.dma_start(out_rows[i], pages[i][:])
+            if i != PAGE_ORDER[3]:
+                nc.scalar.copy(rounded[:, :, i], pages[i][:])
+                return
             for c in range(OUT_CHUNKS):
-                src = pages[i][:, c * OUT_CHUNK : (c + 1) * OUT_CHUNK]
-                if i == 3 and c < VECTOR_ROUNDS:
-                    nc.vector.tensor_copy(rounded[c][:, :, i], src)
+                cols = slice(c * OUT_CHUNK, (c + 1) * OUT_CHUNK)
+                if c < VECTOR_ROUNDS:
+                    nc.vector.tensor_copy(rounded[:, cols, i], pages[i][:, cols])
                 else:
-                    nc.scalar.copy(rounded[c][:, :, i], src)
+                    nc.scalar.copy(rounded[:, cols, i], pages[i][:, cols])
 
-        add_state(PAGE_ORDER[0])
-        for n, i in enumerate(PAGE_ORDER):
-            if n + 1 < 4:
-                add_state(PAGE_ORDER[n + 1])
-            place(i)
+        for c in range(CHUNKS):
+            for i in PAGE_ORDER[:3]:
+                add_state(i, c * CHUNK, CHUNK)
+        place(PAGE_ORDER[0])
+        place(PAGE_ORDER[1])
+        last = PAGE_ORDER[3]
+        total[last] = keep.tile([P, J], F32, name=f"total{last}", tag="total_slot1")
+        add_state(last, 0, J)
+        place(PAGE_ORDER[2])
+        place(last)
 
         out_plane = keep.tile([P, T], U8, name="out_plane", align_bytes=64)
         out_words = out_1[0].rearrange("p t i -> p (t i)").bitcast(I32)
@@ -235,7 +252,7 @@ def tile_list_msg_none_resLP_kernel(
             nc.vector.quantize_mx(
                 out=out_codes[:].bitcast(FP8X4),
                 scales=out_plane[:, cols],
-                in_=rounded[c][:].rearrange("p t i -> p (t i)"),
+                in_=rounded[:, cols, :].rearrange("p t i -> p (t i)"),
             )
             nc.sync.dma_start(out_words[:, cols], out_codes[:].bitcast(I32))
         for q in range(4):

@@ -25,6 +25,7 @@ OUT_CHUNK = 512
 OUT_CHUNKS = T // OUT_CHUNK
 VECTOR_ROUNDS = 2
 PAGE_ORDER = (2, 0, 1, 3)
+HELD = {(0, 0): "tab_plane", (3, 1): "h_bf0"}
 
 
 def tile_list_msg_none_resLP_kernel(
@@ -34,7 +35,7 @@ def tile_list_msg_none_resLP_kernel(
     nc = tc.nc
     with ExitStack() as ctx:
         keep = ctx.enter_context(tc.tile_pool(name="keep", bufs=1))
-        ring = ctx.enter_context(tc.tile_pool(name="ring", bufs=2))
+        ring = ctx.enter_context(tc.tile_pool(name="ring", bufs=CHUNKS))
         psum_a = ctx.enter_context(tc.psum_pool(name="psum_a", bufs=4))
         psum_y = ctx.enter_context(tc.psum_pool(name="psum_y", bufs=4))
 
@@ -44,7 +45,7 @@ def tile_list_msg_none_resLP_kernel(
         for plane in (tab_plane, *w_plane_raw, dst_plane_1):
             nc.vector.memset(plane[:].bitcast(I32), 0)
         pages = {}
-        for n, i in enumerate(PAGE_ORDER[:2]):
+        for n, i in enumerate(PAGE_ORDER[:1]):
             pages[i] = keep.tile([P, T], F32, name=f"page{i}", tag=f"page_slot{n}")
             nc.vector.memset(pages[i][:].bitcast(I32), 0)
 
@@ -53,30 +54,36 @@ def tile_list_msg_none_resLP_kernel(
         nc.sync.dma_start(dst_list[:], offs2)
         nc.sync.dma_start(src_list[:], offs)
 
-        tab = [keep.tile([P, T], U32, name=f"tab{a}", align_bytes=64) for a in range(PASSES)]
+        ws_raw = keep.tile([P, PASSES, R], U32, name="ws_raw")
+        wt_raw = keep.tile([P, PASSES, R // 2], U32, name="wt_raw")
+        wd_raw = keep.tile([P, 4, N], F32, name="wd_raw")
+        tab = keep.tile([P, PASSES * T], U32, name="tab", align_bytes=64)
+        wd_rows = wd.rearrange("(q i u) n -> i q u n", i=4, u=8)
 
-        def load_tab(a):
-            nc.sync.dma_start(tab[a][:].bitcast(I32), tab_words[a].rearrange("p t i -> p (t i)").bitcast(I32))
+        def load_w_plane(w, scales):
+            for q in range(4):
+                nc.sync.dma_start(
+                    w_plane_raw[w][32 * q : 32 * q + 4, :].bitcast(I32).rearrange("p (a r) -> p a r", a=PASSES),
+                    scales[:, 4 * q : 4 * q + 4, :].bitcast(I32).rearrange("a q r -> q a r"),
+                )
 
-        load_tab(0)
+        nc.sync.dma_start(wt_raw[:].bitcast(I32), wt_words.rearrange("a p b -> p a b").bitcast(I32))
         for q in range(4):
             nc.sync.dma_start(
                 tab_plane[32 * q : 32 * q + 4 * PASSES, :].bitcast(I32),
                 tab_scales[:, 4 * q : 4 * q + 4, :].bitcast(I32),
             )
-
-        ws_raw = keep.tile([P, PASSES, R], U32, name="ws_raw")
-        wt_raw = keep.tile([P, PASSES, R // 2], U32, name="wt_raw")
+        nc.sync.dma_start(
+            tab[:].bitcast(I32).rearrange("p (a t) -> p a t", a=PASSES),
+            tab_words.rearrange("a p t i -> p a (t i)").bitcast(I32),
+        )
         nc.sync.dma_start(ws_raw[:].bitcast(I32), ws_words.rearrange("a p r i -> p a (r i)").bitcast(I32))
-        nc.sync.dma_start(wt_raw[:].bitcast(I32), wt_words.rearrange("a p b -> p a b").bitcast(I32))
-        for w, scales in enumerate((ws_scales, wt_scales)):
-            for q in range(4):
-                if (w, q) == (1, 2):
-                    load_tab(1)
-                nc.sync.dma_start(
-                    w_plane_raw[w][32 * q : 32 * q + 4, :].bitcast(I32).rearrange("p (a r) -> p a r", a=PASSES),
-                    scales[:, 4 * q : 4 * q + 4, :].bitcast(I32).rearrange("a q r -> q a r"),
-                )
+        load_w_plane(0, ws_scales)
+        for i in range(2):
+            nc.sync.dma_start(wd_raw[:, i, :], wd_rows[i])
+        load_w_plane(1, wt_scales)
+        for i in range(2, 4):
+            nc.sync.dma_start(wd_raw[:, i, :], wd_rows[i])
 
         dst_plane = keep.tile([P, J], U8, name="dst_plane", align_bytes=64)
         src_plane = keep.tile([P, J], U8, name="src_plane", align_bytes=64)
@@ -84,19 +91,13 @@ def tile_list_msg_none_resLP_kernel(
 
         def pick(c, a):
             offsets = slice(c * CHUNK // 16, (c + 1) * CHUNK // 16)
-            width = 2 * PASSES * CHUNK
-            if a == 0 and c == 1:
-                middle = keep.tile([P, 2 * width], U32, name="picked_middle", tag="tab_plane", align_bytes=64)
-                picked[1], picked[2] = middle[:, :width], middle[:, width:]
-            elif a == 0 and c != 2:
-                tag = "h_bf0" if c == CHUNKS - 1 else "picked_first"
-                picked[c] = keep.tile([P, width], U32, name=f"picked{c}", tag=tag, align_bytes=64)
+            tag = HELD.get((c, a), f"picked{c}_{a}")
+            both = keep.tile([P, 2 * CHUNK], U32, name=f"picked{c}_{a}", tag=tag, align_bytes=64)
             for n, (side, lst) in enumerate((("src", src_list), ("dst", dst_list))):
-                g = picked[c][:, (2 * a + n) * CHUNK : (2 * a + n + 1) * CHUNK]
-                nc.vector.tensor_copy(g, tab[a][:].indirect(lst[:, offsets]))
+                g = both[:, n * CHUNK : (n + 1) * CHUNK]
+                nc.vector.tensor_copy(g, tab[:, a * T : (a + 1) * T].indirect(lst[:, offsets]))
                 picked[side, a, c] = g
 
-        pick(0, 0)
         nc.vector.tensor_copy(dst_plane[:], tab_plane[:].indirect(dst_list[:]))
         nc.vector.tensor_copy(src_plane[:], tab_plane[:].indirect(src_list[:]))
         for q in range(4):
@@ -105,17 +106,14 @@ def tile_list_msg_none_resLP_kernel(
                 dst_plane[32 * q + 4 : 32 * q + 8, :].bitcast(I32),
             )
 
-        wd_raw = keep.tile([P, 4, N], F32, name="wd_raw")
-        wd_rows = wd.rearrange("(q i u) n -> i q u n", i=4, u=8)
-        for i in range(4):
-            nc.sync.dma_start(wd_raw[:, i, :], wd_rows[i])
         wgo_sb = keep.tile([P, J], F32, name="wgo_sb")
         res = [keep.tile([P, T], F32, name=f"res{i}", tag=f"res_slot{i}") for i in range(4)]
         res_rows = rT.rearrange("(p i) t -> i p t", i=4)
-        for i in PAGE_ORDER[:3]:
+        for i in PAGE_ORDER[:2]:
             nc.sync.dma_start(res[i][:], res_rows[i])
         nc.sync.dma_start(wgo_sb[:], wgo)
-        nc.sync.dma_start(res[PAGE_ORDER[3]][:], res_rows[PAGE_ORDER[3]])
+        for i in PAGE_ORDER[2:]:
+            nc.sync.dma_start(res[i][:], res_rows[i])
 
         ws_codes = keep.tile([P, PASSES, R], U32, name="ws_codes", align_bytes=64)
         wt_codes = keep.tile([P, PASSES, R // 2], U32, name="wt_codes", align_bytes=64)
@@ -142,15 +140,14 @@ def tile_list_msg_none_resLP_kernel(
         nc.vector.quantize_mx(out=wd_codes[:].bitcast(FP8X4), scales=wd_plane[:], in_=wd_bf[:])
 
         y = keep.tile([P, 4, J], F32, name="y")
-        total = {i: keep.tile([P, J], F32, name=f"total{i}", tag=f"total_slot{n}") for n, i in enumerate(PAGE_ORDER[:3])}
+        total = {i: keep.tile([P, J], F32, name=f"total{i}", tag=f"total_slot{n}") for n, i in enumerate(PAGE_ORDER[:2])}
 
         def first_stage(c):
             for a in range(PASSES):
-                if ("src", a, c) not in picked:
-                    pick(c, a)
+                pick(c, a)
             h_bf = keep.tile([P, 4 * CHUNK], BF16, name=f"h_bf{c}", tag=f"h_bf{c}", align_bytes=64)
             banks = [psum_a.tile([P, 4, SUB], F32, name="acc") for b in range(CHUNK // SUB)]
-            steps = [(a, side) for a in range(PASSES) for side in ("src", "dst")]
+            steps = [(a, side) for side in ("src", "dst") for a in range(PASSES)]
             for n, (a, side) in enumerate(steps):
                 for b, acc in enumerate(banks):
                     cols = slice(b * SUB, (b + 1) * SUB)
@@ -180,10 +177,13 @@ def tile_list_msg_none_resLP_kernel(
                 )
             return h_bf
 
-        def second_stage(c, h_bf):
+        def quantise_h(h_bf):
             h_codes = ring.tile([P, CHUNK], U32, name="h_codes", align_bytes=64)
             h_plane = ring.tile([P, CHUNK], U8, name="h_plane", align_bytes=64)
             nc.vector.quantize_mx(out=h_codes[:].bitcast(FP8X4), scales=h_plane[:], in_=h_bf[:])
+            return h_codes, h_plane
+
+        def second_stage(c, h_codes, h_plane):
             edges = slice(c * CHUNK, (c + 1) * CHUNK)
             for pair in range(2):
                 acc = psum_y.tile([P, 2, CHUNK], F32, name="acc_y")
@@ -200,13 +200,14 @@ def tile_list_msg_none_resLP_kernel(
                     )
                 nc.scalar.copy(y[:, 2 * pair : 2 * pair + 2, edges], acc[:])
 
-        pending = None
-        for c in range(CHUNKS):
-            h_bf = first_stage(c)
-            if pending is not None:
-                second_stage(*pending)
-            pending = (c, h_bf)
-        second_stage(*pending)
+        h_bf, h_mx = {}, {}
+        for step in range(CHUNKS + 2):
+            if step < CHUNKS:
+                h_bf[step] = first_stage(step)
+            if step >= 2:
+                second_stage(step - 2, *h_mx[step - 2])
+            if 1 <= step <= CHUNKS:
+                h_mx[step - 1] = quantise_h(h_bf[step - 1])
 
         def add_state(i, first, count):
             edges = slice(first, first + count)
@@ -216,12 +217,17 @@ def tile_list_msg_none_resLP_kernel(
         rounded = keep.tile([P, T, 4], BF16, name="rounded", align_bytes=64)
         out_rows = out_0.rearrange("(p i) t -> i p t", i=4)
 
-        def place(i):
+        def scatter(i, first, count):
+            edges = slice(first, first + count)
+            offsets = slice(first // 16, (first + count) // 16)
+            nc.vector.tensor_tensor(pages[i][:].indirect(dst_list[:, offsets]), total[i][:, edges], wgo_sb[:, edges], MULT)
+
+        def place(i, first=0):
             if i not in pages:
-                slot = "page_slot0" if i == PAGE_ORDER[3] else f"res_slot{PAGE_ORDER[0]}"
+                slot = "page_slot0" if i == PAGE_ORDER[3] else f"res_slot{PAGE_ORDER[PAGE_ORDER.index(i) - 1]}"
                 pages[i] = keep.tile([P, T], F32, name=f"page{i}", tag=slot)
                 nc.gpsimd.memset(pages[i][:], 0.0)
-            nc.vector.tensor_tensor(pages[i][:].indirect(dst_list[:]), total[i][:], wgo_sb[:], MULT)
+            scatter(i, first, J - first)
             nc.sync.dma_start(out_rows[i], pages[i][:])
             if i != PAGE_ORDER[3]:
                 nc.scalar.copy(rounded[:, :, i], pages[i][:])
@@ -234,15 +240,17 @@ def tile_list_msg_none_resLP_kernel(
                     nc.scalar.copy(rounded[:, cols, i], pages[i][:, cols])
 
         for c in range(CHUNKS):
-            for i in PAGE_ORDER[:3]:
+            for i in PAGE_ORDER[:2]:
                 add_state(i, c * CHUNK, CHUNK)
-        place(PAGE_ORDER[0])
+            if c == 1:
+                scatter(PAGE_ORDER[0], 0, J // 2)
+        place(PAGE_ORDER[0], J // 2)
         place(PAGE_ORDER[1])
-        last = PAGE_ORDER[3]
-        total[last] = keep.tile([P, J], F32, name=f"total{last}", tag="total_slot1")
-        add_state(last, 0, J)
-        place(PAGE_ORDER[2])
-        place(last)
+        for n, i in enumerate(PAGE_ORDER[2:]):
+            total[i] = keep.tile([P, J], F32, name=f"total{i}", tag=f"total_slot{n}")
+            add_state(i, 0, J)
+        for i in PAGE_ORDER[2:]:
+            place(i)
 
         out_plane = keep.tile([P, T], U8, name="out_plane", align_bytes=64)
         out_words = out_1[0].rearrange("p t i -> p (t i)").bitcast(I32)

@@ -109,10 +109,9 @@ def tile_list_msg_none_resLP_kernel(
         wgo_sb = keep.tile([P, J], F32, name="wgo_sb")
         res = [keep.tile([P, T], F32, name=f"res{i}", tag=f"res_slot{i}") for i in range(4)]
         res_rows = rT.rearrange("(p i) t -> i p t", i=4)
-        for i in PAGE_ORDER[:2]:
-            nc.sync.dma_start(res[i][:], res_rows[i])
+        nc.sync.dma_start(res[PAGE_ORDER[0]][:], res_rows[PAGE_ORDER[0]])
         nc.sync.dma_start(wgo_sb[:], wgo)
-        for i in PAGE_ORDER[2:]:
+        for i in PAGE_ORDER[1:]:
             nc.sync.dma_start(res[i][:], res_rows[i])
 
         ws_codes = keep.tile([P, PASSES, R], U32, name="ws_codes", align_bytes=64)
@@ -240,11 +239,12 @@ def tile_list_msg_none_resLP_kernel(
                     nc.scalar.copy(rounded[:, cols, i], pages[i][:, cols])
 
         for c in range(CHUNKS):
-            for i in PAGE_ORDER[:2]:
-                add_state(i, c * CHUNK, CHUNK)
-            if c == 1:
-                scatter(PAGE_ORDER[0], 0, J // 2)
-        place(PAGE_ORDER[0], J // 2)
+            add_state(PAGE_ORDER[0], c * CHUNK, CHUNK)
+            if c % 2 == 1:
+                add_state(PAGE_ORDER[1], (c - 1) * CHUNK, 2 * CHUNK)
+            if c < CHUNKS - 1:
+                scatter(PAGE_ORDER[0], c * CHUNK, CHUNK)
+        place(PAGE_ORDER[0], J - CHUNK)
         place(PAGE_ORDER[1])
         for n, i in enumerate(PAGE_ORDER[2:]):
             total[i] = keep.tile([P, J], F32, name=f"total{i}", tag=f"total_slot{n}")

from contextlib import ExitStack

import concourse.mybir as mybir

K, R, N, T, J = 1024, 512, 512, 2048, 1024
FLOPS = 2 * (2 * K * R * J + R * N * J)

F32 = mybir.dt.float32
BF16 = mybir.dt.bfloat16
I32 = mybir.dt.int32
U32 = mybir.dt.uint32
U16 = mybir.dt.uint16
U8 = mybir.dt.uint8
FP8X4 = mybir.dt.float8_e4m3fn_x4
FP4X4 = mybir.dt.float4_e2m1fn_x4
ADD = mybir.AluOpType.add
MULT = mybir.AluOpType.mult

P = 128
PASSES = K // 512
CHUNK = 256
CHUNKS = J // CHUNK
SUB = 128
OUT_CHUNK = 512
OUT_CHUNKS = T // OUT_CHUNK
VECTOR_ROUNDS = 2
PAGE_ORDER = (2, 0, 1, 3)
HELD = {(0, 0): "tab_plane", (3, 1): "h_bf0"}


def tile_list_msg_none_resLP_kernel(
    tc, tab_words, tab_scales, ws_words, ws_scales, wt_words, wt_scales, wd, rT, wgo, offs, offs2,
    out_0, out_1, out_2,
):
    nc = tc.nc
    with ExitStack() as ctx:
        keep = ctx.enter_context(tc.tile_pool(name="keep", bufs=1))
        ring = ctx.enter_context(tc.tile_pool(name="ring", bufs=CHUNKS))
        psum_a = ctx.enter_context(tc.psum_pool(name="psum_a", bufs=4))
        psum_y = ctx.enter_context(tc.psum_pool(name="psum_y", bufs=4))

        tab_plane = keep.tile([P, T], U8, name="tab_plane", tag="tab_plane", align_bytes=64)
        w_plane_raw = [keep.tile([P, PASSES * R], U8, name=f"w_plane_raw{w}", align_bytes=64) for w in range(2)]
        dst_plane_1 = keep.tile([P, J], U8, name="dst_plane_1", align_bytes=64)
        for plane in (tab_plane, *w_plane_raw, dst_plane_1):
            nc.vector.memset(plane[:].bitcast(I32), 0)
        pages = {}
        for n, i in enumerate(PAGE_ORDER[:1]):
            pages[i] = keep.tile([P, T], F32, name=f"page{i}", tag=f"page_slot{n}")
            nc.vector.memset(pages[i][:].bitcast(I32), 0)

        dst_list = keep.tile([P, J // 16], U16, name="dst_list")
        src_list = keep.tile([P, J // 16], U16, name="src_list")
        nc.sync.dma_start(dst_list[:], offs2)
        nc.sync.dma_start(src_list[:], offs)

        ws_raw = keep.tile([P, PASSES, R], U32, name="ws_raw")
        wt_raw = keep.tile([P, PASSES, R // 2], U32, name="wt_raw")
        wd_raw = keep.tile([P, 4, N], F32, name="wd_raw")
        tab = keep.tile([P, PASSES * T], U32, name="tab", align_bytes=64)
        wd_rows = wd.rearrange("(q i u) n -> i q u n", i=4, u=8)

        def load_w_plane(w, scales):
            for q in range(4):
                nc.sync.dma_start(
                    w_plane_raw[w][32 * q : 32 * q + 4, :].bitcast(I32).rearrange("p (a r) -> p a r", a=PASSES),
                    scales[:, 4 * q : 4 * q + 4, :].bitcast(I32).rearrange("a q r -> q a r"),
                )

        nc.sync.dma_start(wt_raw[:].bitcast(I32), wt_words.rearrange("a p b -> p a b").bitcast(I32))
        for q in range(4):
            nc.sync.dma_start(
                tab_plane[32 * q : 32 * q + 4 * PASSES, :].bitcast(I32),
                tab_scales[:, 4 * q : 4 * q + 4, :].bitcast(I32),
            )
        nc.sync.dma_start(
            tab[:].bitcast(I32).rearrange("p (a t) -> p a t", a=PASSES),
            tab_words.rearrange("a p t i -> p a (t i)").bitcast(I32),
        )
        nc.sync.dma_start(ws_raw[:].bitcast(I32), ws_words.rearrange("a p r i -> p a (r i)").bitcast(I32))
        load_w_plane(0, ws_scales)
        for i in range(2):
            nc.sync.dma_start(wd_raw[:, i, :], wd_rows[i])
        load_w_plane(1, wt_scales)
        for i in range(2, 4):
            nc.sync.dma_start(wd_raw[:, i, :], wd_rows[i])

        dst_plane = keep.tile([P, J], U8, name="dst_plane", align_bytes=64)
        src_plane = keep.tile([P, J], U8, name="src_plane", align_bytes=64)
        picked = {}

        def pick(c, a):
            offsets = slice(c * CHUNK // 16, (c + 1) * CHUNK // 16)
            tag = HELD.get((c, a), f"picked{c}_{a}")
            both = keep.tile([P, 2 * CHUNK], U32, name=f"picked{c}_{a}", tag=tag, align_bytes=64)
            for n, (side, lst) in enumerate((("src", src_list), ("dst", dst_list))):
                g = both[:, n * CHUNK : (n + 1) * CHUNK]
                nc.vector.tensor_copy(g, tab[:, a * T : (a + 1) * T].indirect(lst[:, offsets]))
                picked[side, a, c] = g

        nc.vector.tensor_copy(dst_plane[:], tab_plane[:].indirect(dst_list[:]))
        nc.vector.tensor_copy(src_plane[:], tab_plane[:].indirect(src_list[:]))
        for q in range(4):
            nc.sync.dma_start(
                dst_plane_1[32 * q : 32 * q + 4, :].bitcast(I32),
                dst_plane[32 * q + 4 : 32 * q + 8, :].bitcast(I32),
            )

        wgo_sb = keep.tile([P, J], F32, name="wgo_sb")
        res = [keep.tile([P, T], F32, name=f"res{i}", tag=f"res_slot{i}") for i in range(4)]
        res_rows = rT.rearrange("(p i) t -> i p t", i=4)
        nc.sync.dma_start(res[PAGE_ORDER[0]][:], res_rows[PAGE_ORDER[0]])
        nc.sync.dma_start(wgo_sb[:], wgo)
        for i in PAGE_ORDER[1:]:
            nc.sync.dma_start(res[i][:], res_rows[i])

        ws_codes = keep.tile([P, PASSES, R], U32, name="ws_codes", align_bytes=64)
        wt_codes = keep.tile([P, PASSES, R // 2], U32, name="wt_codes", align_bytes=64)
        w_plane = [keep.tile([P, PASSES * R], U8, name=f"w_plane{w}", align_bytes=64) for w in range(2)]
        for w, (codes, raw) in enumerate(((ws_codes, ws_raw), (wt_codes, wt_raw))):
            nc.scalar.copy(
                codes[:].rearrange("p a (i q u) -> p a i q u", i=4, q=16),
                raw[:].rearrange("p a (q i u) -> p a i q u", i=4, q=16),
            )
            nc.scalar.copy(
                w_plane[w][:].bitcast(U32).rearrange("p (a i q u) -> p a i q u", a=PASSES, i=4, q=16),
                w_plane_raw[w][:].bitcast(U32).rearrange("p (a q i u) -> p a i q u", a=PASSES, i=4, q=16),
            )

        wd_bf = keep.tile([P, 4 * N], BF16, name="wd_bf", align_bytes=64)
        wd_codes = keep.tile([P, N], U32, name="wd_codes", align_bytes=64)
        wd_plane = keep.tile([P, N], U8, name="wd_plane", align_bytes=64)
        for half in range(2):
            ms = slice(half * P // 2, (half + 1) * P // 2)
            nc.scalar.copy(
                wd_bf[:].rearrange("p (s m i) -> p m s i", s=4, i=4)[:, ms],
                wd_raw[:].rearrange("p i (m s) -> p m s i", s=4)[:, ms],
            )
        nc.vector.quantize_mx(out=wd_codes[:].bitcast(FP8X4), scales=wd_plane[:], in_=wd_bf[:])

        y = keep.tile([P, 4, J], F32, name="y")
        total = {i: keep.tile([P, J], F32, name=f"total{i}", tag=f"total_slot{n}") for n, i in enumerate(PAGE_ORDER[:2])}

        def first_stage(c):
            for a in range(PASSES):
                pick(c, a)
            h_bf = keep.tile([P, 4 * CHUNK], BF16, name=f"h_bf{c}", tag=f"h_bf{c}", align_bytes=64)
            banks = [psum_a.tile([P, 4, SUB], F32, name="acc") for b in range(CHUNK // SUB)]
            steps = [(a, side) for side in ("src", "dst") for a in range(PASSES)]
            for n, (a, side) in enumerate(steps):
                for b, acc in enumerate(banks):
                    cols = slice(b * SUB, (b + 1) * SUB)
                    edges = slice(c * CHUNK + b * SUB, c * CHUNK + (b + 1) * SUB)
                    for i in range(4):
                        if side == "src":
                            lhsT = ws_codes[:, a, i * P : (i + 1) * P].bitcast(FP8X4)
                            lhsT_plane = w_plane[0]
                            rhs_scale = src_plane[4 * a : P, edges]
                        else:
                            lhsT = wt_codes[:, a, i * P // 2 : (i + 1) * P // 2].bitcast(U8).bitcast(FP4X4)
                            lhsT_plane = w_plane[1]
                            rhs_scale = (dst_plane, dst_plane_1)[a][:, edges]
                        nc.tensor.matmul_mx(
                            out=acc[:, i, :],
                            lhsT=lhsT,
                            lhsT_scale=lhsT_plane[:, a * R + i * P : a * R + (i + 1) * P],
                            rhs=picked[side, a, c][:, cols].bitcast(FP8X4),
                            rhs_scale=rhs_scale,
                            start=(n == 0 and i == 0),
                            stop=(n == len(steps) - 1 and i == 3),
                        )
            for b, acc in enumerate(banks):
                nc.scalar.copy(
                    h_bf[:, 4 * b * SUB : 4 * (b + 1) * SUB].rearrange("p (j i) -> p j i", i=4),
                    acc[:].rearrange("p i j -> p j i"),
                )
            return h_bf

        def quantise_h(h_bf):
            h_codes = ring.tile([P, CHUNK], U32, name="h_codes", align_bytes=64)
            h_plane = ring.tile([P, CHUNK], U8, name="h_plane", align_bytes=64)
            nc.vector.quantize_mx(out=h_codes[:].bitcast(FP8X4), scales=h_plane[:], in_=h_bf[:])
            return h_codes, h_plane

        def second_stage(c, h_codes, h_plane):
            edges = slice(c * CHUNK, (c + 1) * CHUNK)
            for pair in range(2):
                acc = psum_y.tile([P, 2, CHUNK], F32, name="acc_y")
                for s in range(2):
                    i = PAGE_ORDER[2 * pair + s]
                    nc.tensor.matmul_mx(
                        out=acc[:, s, :],
                        lhsT=wd_codes[:, i * P : (i + 1) * P].bitcast(FP8X4),
                        lhsT_scale=wd_plane[:, i * P : (i + 1) * P],
                        rhs=h_codes[:].bitcast(FP8X4),
                        rhs_scale=h_plane[:],
                        start=True,
                        stop=True,
                    )
                nc.scalar.copy(y[:, 2 * pair : 2 * pair + 2, edges], acc[:])

        h_bf, h_mx = {}, {}
        for step in range(CHUNKS + 2):
            if step < CHUNKS:
                h_bf[step] = first_stage(step)
            if step >= 2:
                second_stage(step - 2, *h_mx[step - 2])
            if 1 <= step <= CHUNKS:
                h_mx[step - 1] = quantise_h(h_bf[step - 1])

        def add_state(i, first, count):
            edges = slice(first, first + count)
            offsets = slice(first // 16, (first + count) // 16)
            nc.vector.tensor_tensor(total[i][:, edges], res[i][:].indirect(dst_list[:, offsets]), y[:, PAGE_ORDER.index(i), edges], ADD)

        rounded = keep.tile([P, T, 4], BF16, name="rounded", align_bytes=64)
        out_rows = out_0.rearrange("(p i) t -> i p t", i=4)

        def scatter(i, first, count):
            edges = slice(first, first + count)
            offsets = slice(first // 16, (first + count) // 16)
            nc.vector.tensor_tensor(pages[i][:].indirect(dst_list[:, offsets]), total[i][:, edges], wgo_sb[:, edges], MULT)

        def place(i, first=0):
            if i not in pages:
                slot = "page_slot0" if i == PAGE_ORDER[3] else f"res_slot{PAGE_ORDER[PAGE_ORDER.index(i) - 1]}"
                pages[i] = keep.tile([P, T], F32, name=f"page{i}", tag=slot)
                nc.gpsimd.memset(pages[i][:], 0.0)
            scatter(i, first, J - first)
            nc.sync.dma_start(out_rows[i], pages[i][:])
            if i != PAGE_ORDER[3]:
                nc.scalar.copy(rounded[:, :, i], pages[i][:])
                return
            for c in range(OUT_CHUNKS):
                cols = slice(c * OUT_CHUNK, (c + 1) * OUT_CHUNK)
                if c < VECTOR_ROUNDS:
                    nc.vector.tensor_copy(rounded[:, cols, i], pages[i][:, cols])
                else:
                    nc.scalar.copy(rounded[:, cols, i], pages[i][:, cols])

        for c in range(CHUNKS):
            add_state(PAGE_ORDER[0], c * CHUNK, CHUNK)
            if c % 2 == 1:
                add_state(PAGE_ORDER[1], (c - 1) * CHUNK, 2 * CHUNK)
            if c < CHUNKS - 1:
                scatter(PAGE_ORDER[0], c * CHUNK, CHUNK)
        place(PAGE_ORDER[0], J - CHUNK)
        place(PAGE_ORDER[1])
        for n, i in enumerate(PAGE_ORDER[2:]):
            total[i] = keep.tile([P, J], F32, name=f"total{i}", tag=f"total_slot{n}")
            add_state(i, 0, J)
        for i in PAGE_ORDER[2:]:
            place(i)

        out_plane = keep.tile([P, T], U8, name="out_plane", align_bytes=64)
        out_words = out_1[0].rearrange("p t i -> p (t i)").bitcast(I32)
        for c in range(OUT_CHUNKS):
            cols = slice(c * OUT_CHUNK, (c + 1) * OUT_CHUNK)
            out_codes = keep.tile([P, OUT_CHUNK], U32, name=f"out_codes{c}", align_bytes=64)
            nc.vector.quantize_mx(
                out=out_codes[:].bitcast(FP8X4),
                scales=out_plane[:, cols],
                in_=rounded[:, cols, :].rearrange("p t i -> p (t i)"),
            )
            nc.sync.dma_start(out_words[:, cols], out_codes[:].bitcast(I32))
        for q in range(4):
            nc.scalar.dma_start(
                out_2[0, 4 * q : 4 * q + 4, :].bitcast(I32),
                out_plane[32 * q : 32 * q + 4, :].bitcast(I32),
            )
